import numpy as np
import ml_dtypes


def mxq(x, axis, fmt="e4m3"):
    dtype, down = {"e4m3": (ml_dtypes.float8_e4m3fn, 7), "e5m2": (ml_dtypes.float8_e5m2, 14)}[fmt]
    v = np.moveaxis(np.asarray(x, np.float32).astype(ml_dtypes.bfloat16).astype(np.float64), axis, -1)
    blocks = v.reshape(v.shape[:-1] + (-1, 32))
    amax = np.abs(blocks).max(-1, keepdims=True)
    byte = np.maximum(np.where(amax > 0, np.frexp(amax)[1] - 1 + 127, 0) - down, 1)
    scale = np.exp2(byte - 127.0)
    codes = (blocks / scale).astype(np.float32).astype(dtype).astype(np.float64)
    return np.moveaxis((codes * scale).reshape(v.shape), -1, axis)


WIDE = False


def mx_kscale(k):
    if not WIDE:
        return np.ones(k)
    levels = np.array([10, -10, 5, -5, 0])
    if k % 512:
        return np.exp2(np.random.permutation(np.resize(levels, k // 32))).repeat(32)
    a = np.empty((k // 512, 16))
    for p in range(k // 512):
        a[p, :8] = np.random.permutation(np.resize(levels, 8))
        for g in range(8):
            far = levels[np.abs(levels - a[p, g]) >= 10]
            a[p, g + 8] = far[np.random.randint(len(far))]
    return np.exp2(a.ravel()).repeat(32)


def f64(x):
    return np.asarray(x).astype(np.float64)


def striped8(idx):
    return np.asarray(idx).reshape(8, -1, 16).transpose(0, 2, 1).reshape(128, -1).astype(np.uint16)


def unstriped8(offs):
    return offs.reshape(8, 16, -1).transpose(0, 2, 1).reshape(8, -1).astype(np.int64)


def pick8(x, idx, run):
    r = np.arange(len(x))
    return x[r[:, None], idx[r % (8 * run) // run]]


E2M1 = np.array([0.0, 0.5, 1.0, 1.5, 2.0, 3.0, 4.0, 6.0, -0.0, -0.5, -1.0, -1.5, -2.0, -3.0, -4.0, -6.0])


def pack_weight(w, fmt):
    k, n = w.shape
    w = f64(np.asarray(w, np.float32).astype(ml_dtypes.bfloat16)).reshape(k // 32, 32, n)
    amax = np.abs(w).max(1)
    if fmt == "e4m3":
        byte = np.frexp(amax)[1] - 1 + 127 - 7
    else:
        mant, ex = np.frexp(amax / 6.0)
        byte = np.where(mant > 0.5, ex, ex - 1) + 127
    byte = np.clip(np.where(amax > 0, byte, 1), 1, 254)
    scaled = (w * np.exp2(127.0 - byte)[:, None, :]).reshape(k, n).astype(np.float32)
    by_word = np.ascontiguousarray(scaled.reshape(k // 512, 128, 4, n).transpose(0, 1, 3, 2))
    if fmt == "e4m3":
        words = by_word.astype(ml_dtypes.float8_e4m3fn).view(np.uint8)
    else:
        c = by_word.astype(ml_dtypes.float4_e2m1fn).view(np.uint8) & 0xF
        words = (c[..., 0::2] | (c[..., 1::2] << 4)).reshape(k // 512, 128, 2 * n)
    return np.ascontiguousarray(words), np.ascontiguousarray(byte.astype(np.uint8).reshape(k // 512, 16, n))


def unpack_weight(words, scales, fmt):
    g, _, n = scales.shape
    words = np.ascontiguousarray(words).reshape(g, 128, n, -1)
    if fmt == "e4m3":
        vals = words.view(ml_dtypes.float8_e4m3fn).astype(np.float64)
    else:
        nib = np.empty((g, 128, n, 4), np.uint8)
        nib[..., 0::2] = words & 0xF
        nib[..., 1::2] = words >> 4
        vals = E2M1[nib]
    vals = vals * np.repeat(np.exp2(scales.astype(np.float64) - 127.0), 8, axis=1)[..., None]
    return vals.transpose(0, 1, 3, 2).reshape(g * 512, n)


def sigmoid(v):
    return 1.0 / (1.0 + np.exp(-v))


def sgn(shape):
    return np.random.uniform(0.5, 2.0, shape) * np.where(np.random.standard_normal(shape) < 0, -1.0, 1.0)


D, K, T, U, I, Q = 512, 512, 1024, 1024, 512, 128


def setup_inputs():
    n = np.random.standard_normal
    idx = np.stack([np.random.permutation(U)[:I] for _ in range(8)])
    idx2 = np.stack([np.random.permutation(T)[:I] for _ in range(8)])
    idx3 = np.stack([np.random.permutation(T)[:I] for _ in range(8)])
    idx4 = np.stack([np.random.permutation(U)[:I] for _ in range(8)])
    idx5 = np.stack([np.random.permutation(U)[:I] for _ in range(8)])
    fd = mx_kscale(D)
    fk = mx_kscale(K)
    wqp = pack_weight(n((D, K)) * 1.0 / np.sqrt(D) * fd[:, None] * fk, "e4m3")
    cachep = pack_weight(n((K, T)) * 1.0 / np.sqrt(K) / fk[:, None], "e2m1")
    draftp = pack_weight(n((D, U)) * 1.0 / np.sqrt(D) * fd[:, None], "e4m3")
    return {
        "states": (n((D, Q)) * 0.95 / fd[:, None]).astype(np.float32),
        "wq_words": wqp[0],
        "wq_scales": wqp[1],
        "cache_words": cachep[0],
        "cache_scales": cachep[1],
        "draft_words": draftp[0],
        "draft_scales": draftp[1],
        "thr": (np.random.uniform(-2.0, 2.0, (Q, 1))).astype(np.float32),
        "slope": (sgn((Q, 1))).astype(np.float32),
        "offs": striped8(idx),
        "offs2": striped8(idx2),
        "offs3": striped8(idx3),
        "offs4": striped8(idx4),
        "offs5": striped8(idx5),
    }


def reference(states, wq_words, wq_scales, cache_words, cache_scales, draft_words, draft_scales, thr, slope, offs, offs2, offs3, offs4, offs5):
    idx = unstriped8(offs)
    idx2 = unstriped8(offs2)
    idx3 = unstriped8(offs3)
    idx4 = unstriped8(offs4)
    idx5 = unstriped8(offs5)
    wqu = unpack_weight(wq_words, wq_scales, "e4m3")
    cacheu = unpack_weight(cache_words, cache_scales, "e2m1")
    draftu = unpack_weight(draft_words, draft_scales, "e4m3")
    statesq = mxq(f64(states), 0, "e4m3")
    qv = wqu.T @ statesq
    qvq = mxq(qv, 0, "e4m3")
    a = qvq.T @ cacheu
    b = statesq.T @ draftu
    s1 = sigmoid(pick8(b, idx, 16) * f64(slope) + f64(thr))
    kp = np.zeros((Q, T))
    kp[np.arange(Q)[:, None], idx2[np.arange(Q) % 128 // 16]] = s1
    aa = a * kp
    v = np.maximum(pick8(aa, idx3, 16), pick8(b, idx4, 16))
    f1 = np.zeros((Q, U))
    f1[np.arange(Q)[:, None], idx4[np.arange(Q) % 128 // 16]] = v
    bb = f1 - b
    y = pick8(bb, idx5, 16)
    return y

@@ -1,0 +1,159 @@
+from contextlib import ExitStack
+
+import concourse.mybir as mybir
+from concourse.masks import make_identity
+
+D, K, T, U, SLOTS, Q = 512, 512, 1024, 1024, 512, 128
+FLOPS = 2 * Q * (D * K + K * T + D * U)
+
+F32 = mybir.dt.float32
+BF16 = mybir.dt.bfloat16
+I32 = mybir.dt.int32
+U32 = mybir.dt.uint32
+U16 = mybir.dt.uint16
+U8 = mybir.dt.uint8
+FP8X4 = mybir.dt.float8_e4m3fn_x4
+FP4X4 = mybir.dt.float4_e2m1fn_x4
+ALU = mybir.AluOpType
+ACT = mybir.ActivationFunctionType
+
+P = 128
+PACK = 4
+LIST_COLS = SLOTS // 16
+BANK = 512
+B_PIECE = 256
+
+
+def load_scale_rows(engine, plane, scales):
+    by_row = scales[0].rearrange("(g r) n -> r g n", r=4)
+    for r in range(4):
+        engine.dma_start(plane[r:P:32, :].bitcast(I32), by_row[r].bitcast(I32))
+
+
+def tile_attend_softkeep_side_kernel(tc, states, wq_words, wq_scales, cache_words, cache_scales, draft_words,
+                                      draft_scales, thr, slope, offs, offs2, offs3, offs4, offs5, out):
+    nc = tc.nc
+    with ExitStack() as ctx:
+        sb = ctx.enter_context(tc.tile_pool(name="sb", bufs=1))
+        ps = ctx.enter_context(tc.psum_pool(name="ps", bufs=1))
+
+        draft_plane = sb.tile([P, U], U8, align_bytes=64)
+        wq_plane = sb.tile([P, K], U8, align_bytes=64)
+        cache_plane = sb.tile([P, T], U8, align_bytes=64)
+        kp = sb.tile([P, T], F32)
+        for plane in (draft_plane, wq_plane, cache_plane):
+            nc.gpsimd.memset(plane[:].bitcast(I32), 0)
+        nc.vector.memset(kp[:], 0.0)
+        ident = sb.tile([P, P], BF16)
+        make_identity(nc, ident[:])
+
+        raw = sb.tile([P, PACK, Q], F32)
+        nc.sync.dma_start(raw[:], states.rearrange("(p j) q -> p j q", j=PACK))
+        load_scale_rows(nc.scalar, draft_plane, draft_scales)
+        draft_rows = draft_words[0].rearrange("p n t -> p (n t)").bitcast(I32)
+        draft = []
+        for h in range(U // BANK):
+            half = sb.tile([P, BANK], U32, align_bytes=64, name="draft%d" % h)
+            nc.sync.dma_start(half[:].bitcast(I32), draft_rows[:, h * BANK : (h + 1) * BANK])
+            draft.append(half)
+        wq = sb.tile([P, K], U32, align_bytes=64)
+        nc.sync.dma_start(wq[:].bitcast(I32), wq_words[0].rearrange("p n t -> p (n t)").bitcast(I32))
+        thr_sb = sb.tile([P, 1], F32)
+        nc.sync.dma_start(thr_sb[:], thr)
+        slope_sb = sb.tile([P, 1], F32)
+        nc.sync.dma_start(slope_sb[:], slope)
+        l1 = sb.tile([P, LIST_COLS], U16)
+        nc.sync.dma_start(l1[:], offs)
+        load_scale_rows(nc.sync, wq_plane, wq_scales)
+        l2 = sb.tile([P, LIST_COLS], U16)
+        nc.sync.dma_start(l2[:], offs2)
+        cache = sb.tile([P, 2 * T], U8, align_bytes=64)
+        nc.sync.dma_start(cache[:].bitcast(I32), cache_words[0].bitcast(I32))
+        load_scale_rows(nc.sync, cache_plane, cache_scales)
+        l4 = sb.tile([P, LIST_COLS], U16)
+        nc.sync.dma_start(l4[:], offs4)
+        l3 = sb.tile([P, LIST_COLS], U16)
+        nc.sync.dma_start(l3[:], offs3)
+        l5 = sb.tile([P, LIST_COLS], U16)
+        nc.sync.dma_start(l5[:], offs5)
+
+        st16 = sb.tile([P, Q, PACK], BF16, align_bytes=64)
+        nc.vector.tensor_copy(st16[:], raw[:].rearrange("p j q -> p q j"))
+        st_codes = sb.tile([P, Q], U32, align_bytes=64)
+        st_plane = sb.tile([P, Q], U8, align_bytes=64)
+        nc.vector.quantize_mx(out=st_codes[:].bitcast(FP8X4), scales=st_plane[:],
+                              in_=st16[:].rearrange("p q j -> p (q j)"))
+
+        b = sb.tile([P, U], F32)
+        b_acc = []
+        for i in range(U // B_PIECE):
+            u0 = i * B_PIECE
+            h, c0 = divmod(u0, BANK)
+            acc = ps.tile([P, B_PIECE], F32, name="b_acc%d" % i)
+            nc.tensor.matmul_mx(out=acc[:], lhsT=st_codes[:].bitcast(FP8X4), lhsT_scale=st_plane[:],
+                                rhs=draft[h][:, c0 : c0 + B_PIECE].bitcast(FP8X4),
+                                rhs_scale=draft_plane[:, u0 : u0 + B_PIECE], start=True, stop=True)
+            nc.vector.tensor_copy(b[:, u0 : u0 + B_PIECE], acc[:])
+            b_acc.append(acc)
+
+        s1 = sb.tile([P, SLOTS], F32)
+        nc.scalar.activation(s1[:], b[:].indirect(l1[:]), ACT.Sigmoid, bias=thr_sb[:], scale=slope_sb[:])
+        nc.scalar.activation(kp[:].indirect(l2[:]), s1[:], ACT.Copy)
+
+        qv_acc = ps.tile([P, K], F32)
+        nc.tensor.matmul_mx(out=qv_acc[:], lhsT=st_codes[:].bitcast(FP8X4), lhsT_scale=st_plane[:],
+                            rhs=wq[:].bitcast(FP8X4), rhs_scale=wq_plane[:], start=True, stop=True)
+        qv_rows = sb.tile([P, PACK, P], BF16)
+        nc.vector.tensor_copy(qv_rows[:], qv_acc[:].rearrange("q (p j) -> q j p", j=PACK))
+        qv_turned = ps.tile([P, PACK, Q], BF16)
+        for j in range(PACK):
+            nc.tensor.transpose(qv_turned[:, j, :], qv_rows[:, j, :], ident[:])
+        qv16 = sb.tile([P, Q, PACK], BF16, align_bytes=64, tag="qv16_then_f1")
+        nc.vector.tensor_copy(qv16[:], qv_turned[:].rearrange("p j q -> p q j"))
+        qv_codes = sb.tile([P, Q], U32, align_bytes=64)
+        qv_plane = sb.tile([P, Q], U8, align_bytes=64)
+        nc.vector.quantize_mx(out=qv_codes[:].bitcast(FP8X4), scales=qv_plane[:],
+                              in_=qv16[:].rearrange("p q j -> p (q j)"))
+        a_acc = []
+        for h in range(T // BANK):
+            acc = ps.tile([P, BANK], F32, name="a_acc%d" % h)
+            nc.tensor.matmul_mx(out=acc[:], lhsT=qv_codes[:].bitcast(FP8X4), lhsT_scale=qv_plane[:],
+                                rhs=cache[:, 2 * h * BANK : 2 * (h + 1) * BANK].bitcast(FP4X4),
+                                rhs_scale=cache_plane[:, h * BANK : (h + 1) * BANK], start=True, stop=True)
+            a_acc.append(acc)
+
+        f1 = sb.tile([P, U], F32, align_bytes=64, tag="qv16_then_f1")
+        nc.vector.memset(f1[:], 0.0)
+
+        half_slots = SLOTS // 2
+        half_cols = LIST_COLS // 2
+        b4 = []
+        for h in range(2):
+            piece = sb.tile([P, half_slots], F32, name="b4_%d" % h)
+            nc.vector.tensor_copy(piece[:], b[:].indirect(l4[:, h * half_cols : (h + 1) * half_cols]))
+            b4.append(piece)
+
+        aa = sb.tile([P, T], F32)
+        for h in range(T // BANK):
+            cols = slice(h * BANK, (h + 1) * BANK)
+            nc.vector.tensor_tensor(aa[:, cols], a_acc[h][:], kp[:, cols], ALU.mult)
+
+        for h in range(2):
+            entries = slice(h * half_cols, (h + 1) * half_cols)
+            a3 = sb.tile([P, half_slots], F32)
+            nc.vector.tensor_copy(a3[:], aa[:].indirect(l3[:, entries]))
+            v = sb.tile([P, half_slots], F32, name="v%d" % h)
+            nc.vector.tensor_tensor(v[:], a3[:], b4[h][:], ALU.max)
+            nc.scalar.activation(f1[:].indirect(l4[:, entries]), v[:], ACT.Copy)
+
+        bb = sb.tile([P, U], F32)
+        for i in range(U // B_PIECE):
+            cols = slice(i * B_PIECE, (i + 1) * B_PIECE)
+            nc.vector.tensor_tensor(bb[:, cols], f1[:, cols], b_acc[i][:], ALU.subtract)
+
+        y0 = sb.tile([P, half_slots], F32)
+        nc.vector.tensor_copy(y0[:], bb[:].indirect(l5[:, 0:half_cols]))
+        nc.sync.dma_start(out[:, 0:half_slots], y0[:])
+        y1 = sb.tile([P, half_slots], F32)
+        nc.scalar.activation(y1[:], bb[:].indirect(l5[:, half_cols:LIST_COLS]), ACT.Copy)
+        nc.scalar.dma_start(out[:, half_slots:SLOTS], y1[:])

@@ -22,11 +22,13 @@ PACK = 4
 LIST_COLS = SLOTS // 16
 BANK = 512
 B_PIECE = 256
+CAST_ON_VECTOR = 72
+ON_GPSIMD = 320
 
 
-def load_scale_rows(engine, plane, scales):
+def load_scale_rows(engines, plane, scales):
     by_row = scales[0].rearrange("(g r) n -> r g n", r=4)
-    for r in range(4):
+    for r, engine in enumerate(engines):
         engine.dma_start(plane[r:P:32, :].bitcast(I32), by_row[r].bitcast(I32))
 
 
@@ -44,47 +46,60 @@ def tile_attend_softkeep_side_kernel(tc, states, wq_words, wq_scales, cache_word
         for plane in (draft_plane, wq_plane, cache_plane):
             nc.gpsimd.memset(plane[:].bitcast(I32), 0)
         nc.vector.memset(kp[:], 0.0)
-        ident = sb.tile([P, P], BF16)
+        f1 = sb.tile([P, U], F32)
+        nc.vector.memset(f1[:], 0.0)
+        ident = sb.tile([P, P], F32)
         make_identity(nc, ident[:])
 
         raw = sb.tile([P, PACK, Q], F32)
         nc.sync.dma_start(raw[:], states.rearrange("(p j) q -> p j q", j=PACK))
-        load_scale_rows(nc.scalar, draft_plane, draft_scales)
+        load_scale_rows((nc.scalar, nc.scalar, nc.sync, nc.sync), draft_plane, draft_scales)
         draft_rows = draft_words[0].rearrange("p n t -> p (n t)").bitcast(I32)
         draft = []
         for h in range(U // BANK):
             half = sb.tile([P, BANK], U32, align_bytes=64, name="draft%d" % h)
             nc.sync.dma_start(half[:].bitcast(I32), draft_rows[:, h * BANK : (h + 1) * BANK])
             draft.append(half)
-        wq = sb.tile([P, K], U32, align_bytes=64)
+        wq_rows = sb.tile([4, 4, K // 4], I32)
+        nc.sync.dma_start(wq_rows[:], wq_scales[0].bitcast(I32).rearrange("(g r) n -> r g n", r=4))
+        wq = sb.tile([P, K], U32, align_bytes=64, tag="wq_then_b4")
         nc.sync.dma_start(wq[:].bitcast(I32), wq_words[0].rearrange("p n t -> p (n t)").bitcast(I32))
+        l1 = sb.tile([P, LIST_COLS], U16)
+        nc.sync.dma_start(l1[:], offs)
         thr_sb = sb.tile([P, 1], F32)
         nc.sync.dma_start(thr_sb[:], thr)
         slope_sb = sb.tile([P, 1], F32)
         nc.sync.dma_start(slope_sb[:], slope)
-        l1 = sb.tile([P, LIST_COLS], U16)
-        nc.sync.dma_start(l1[:], offs)
-        load_scale_rows(nc.sync, wq_plane, wq_scales)
         l2 = sb.tile([P, LIST_COLS], U16)
         nc.sync.dma_start(l2[:], offs2)
-        cache = sb.tile([P, 2 * T], U8, align_bytes=64)
-        nc.sync.dma_start(cache[:].bitcast(I32), cache_words[0].bitcast(I32))
-        load_scale_rows(nc.sync, cache_plane, cache_scales)
         l4 = sb.tile([P, LIST_COLS], U16)
         nc.sync.dma_start(l4[:], offs4)
+        cache = sb.tile([P, 2 * T], U8, align_bytes=64)
+        nc.sync.dma_start(cache[:].bitcast(I32), cache_words[0].bitcast(I32))
+        load_scale_rows((nc.sync,) * 4, cache_plane, cache_scales)
         l3 = sb.tile([P, LIST_COLS], U16)
         nc.sync.dma_start(l3[:], offs3)
         l5 = sb.tile([P, LIST_COLS], U16)
         nc.sync.dma_start(l5[:], offs5)
 
+        warm_in = sb.tile([P, 1], F32)
+        nc.gpsimd.memset(warm_in[:], 0.0)
+        warm_out = sb.tile([P, 1], F32)
+        nc.scalar.activation(warm_out[:], warm_in[:], ACT.Sigmoid)
+
         st16 = sb.tile([P, Q, PACK], BF16, align_bytes=64)
-        nc.vector.tensor_copy(st16[:], raw[:].rearrange("p j q -> p q j"))
+        by_query = raw[:].rearrange("p j q -> p q j")
+        nc.vector.tensor_copy(st16[:, 0:CAST_ON_VECTOR, :], by_query[:, 0:CAST_ON_VECTOR, :])
+        nc.scalar.copy(st16[:, CAST_ON_VECTOR:Q, :], by_query[:, CAST_ON_VECTOR:Q, :])
         st_codes = sb.tile([P, Q], U32, align_bytes=64)
         st_plane = sb.tile([P, Q], U8, align_bytes=64)
         nc.vector.quantize_mx(out=st_codes[:].bitcast(FP8X4), scales=st_plane[:],
                               in_=st16[:].rearrange("p q j -> p (q j)"))
 
-        b = sb.tile([P, U], F32)
+        for g in range(4):
+            nc.vector.tensor_copy(wq_plane[32 * g : 32 * g + 4, :].bitcast(I32), wq_rows[:, g, :])
+
+        b = sb.tile([P, U], F32, tag="b_then_aa")
         b_acc = []
         for i in range(U // B_PIECE):
             u0 = i * B_PIECE
@@ -93,27 +108,36 @@ def tile_attend_softkeep_side_kernel(tc, states, wq_words, wq_scales, cache_word
             nc.tensor.matmul_mx(out=acc[:], lhsT=st_codes[:].bitcast(FP8X4), lhsT_scale=st_plane[:],
                                 rhs=draft[h][:, c0 : c0 + B_PIECE].bitcast(FP8X4),
                                 rhs_scale=draft_plane[:, u0 : u0 + B_PIECE], start=True, stop=True)
-            nc.vector.tensor_copy(b[:, u0 : u0 + B_PIECE], acc[:])
+            copy_out = nc.vector.tensor_copy if i % 2 == 0 else nc.scalar.copy
+            copy_out(b[:, u0 : u0 + B_PIECE], acc[:])
             b_acc.append(acc)
 
         s1 = sb.tile([P, SLOTS], F32)
-        nc.scalar.activation(s1[:], b[:].indirect(l1[:]), ACT.Sigmoid, bias=thr_sb[:], scale=slope_sb[:])
-        nc.scalar.activation(kp[:].indirect(l2[:]), s1[:], ACT.Copy)
+        half_slots = SLOTS // 2
+        half_cols = LIST_COLS // 2
+        for h in range(2):
+            nc.scalar.activation(s1[:, h * half_slots : (h + 1) * half_slots],
+                                 b[:].indirect(l1[:, h * half_cols : (h + 1) * half_cols]),
+                                 ACT.Sigmoid, bias=thr_sb[:], scale=slope_sb[:])
+        for h in range(2):
+            nc.scalar.activation(kp[:].indirect(l2[:, h * half_cols : (h + 1) * half_cols]),
+                                 s1[:, h * half_slots : (h + 1) * half_slots], ACT.Copy)
 
         qv_acc = ps.tile([P, K], F32)
         nc.tensor.matmul_mx(out=qv_acc[:], lhsT=st_codes[:].bitcast(FP8X4), lhsT_scale=st_plane[:],
                             rhs=wq[:].bitcast(FP8X4), rhs_scale=wq_plane[:], start=True, stop=True)
-        qv_rows = sb.tile([P, PACK, P], BF16)
-        nc.vector.tensor_copy(qv_rows[:], qv_acc[:].rearrange("q (p j) -> q j p", j=PACK))
-        qv_turned = ps.tile([P, PACK, Q], BF16)
-        for j in range(PACK):
-            nc.tensor.transpose(qv_turned[:, j, :], qv_rows[:, j, :], ident[:])
-        qv16 = sb.tile([P, Q, PACK], BF16, align_bytes=64, tag="qv16_then_f1")
-        nc.vector.tensor_copy(qv16[:], qv_turned[:].rearrange("p j q -> p q j"))
+        qv_turned = ps.tile([P, 2, Q], F32)
+        for u in range(2):
+            qv_rows = sb.tile([P, P, 2], BF16, name="qv_rows%d" % u)
+            nc.vector.tensor_copy(qv_rows[:], qv_acc[:].rearrange("q (p u e) -> q u p e", u=2, e=2)[:, u])
+            nc.tensor.transpose(qv_turned[:, u, :], qv_rows[:].rearrange("q p e -> q (p e)").bitcast(F32), ident[:])
+        qv16 = sb.tile([P, Q * PACK], BF16, align_bytes=64, tag="qv16_then_b4")
+        nc.vector.tensor_copy(qv16[:].bitcast(F32).rearrange("p (q u) -> p q u", u=2),
+                              qv_turned[:].rearrange("p u q -> p q u"))
         qv_codes = sb.tile([P, Q], U32, align_bytes=64)
         qv_plane = sb.tile([P, Q], U8, align_bytes=64)
         nc.vector.quantize_mx(out=qv_codes[:].bitcast(FP8X4), scales=qv_plane[:],
-                              in_=qv16[:].rearrange("p q j -> p (q j)"))
+                              in_=qv16[:])
         a_acc = []
         for h in range(T // BANK):
             acc = ps.tile([P, BANK], F32, name="a_acc%d" % h)
@@ -122,34 +146,36 @@ def tile_attend_softkeep_side_kernel(tc, states, wq_words, wq_scales, cache_word
                                 rhs_scale=cache_plane[:, h * BANK : (h + 1) * BANK], start=True, stop=True)
             a_acc.append(acc)
 
-        f1 = sb.tile([P, U], F32, align_bytes=64, tag="qv16_then_f1")
-        nc.vector.memset(f1[:], 0.0)
-
-        half_slots = SLOTS // 2
-        half_cols = LIST_COLS // 2
         b4 = []
-        for h in range(2):
-            piece = sb.tile([P, half_slots], F32, name="b4_%d" % h)
+        for h, tag in enumerate(("wq_then_b4", "qv16_then_b4")):
+            piece = sb.tile([P, half_slots], F32, align_bytes=64, name="b4_%d" % h, tag=tag)
             nc.vector.tensor_copy(piece[:], b[:].indirect(l4[:, h * half_cols : (h + 1) * half_cols]))
             b4.append(piece)
 
-        aa = sb.tile([P, T], F32)
-        for h in range(T // BANK):
-            cols = slice(h * BANK, (h + 1) * BANK)
-            nc.vector.tensor_tensor(aa[:, cols], a_acc[h][:], kp[:, cols], ALU.mult)
+        a_head = sb.tile([P, ON_GPSIMD], F32)
+        nc.vector.tensor_copy(a_head[:], a_acc[0][:, 0:ON_GPSIMD])
+        aa = sb.tile([P, T], F32, tag="b_then_aa")
+        nc.gpsimd.tensor_tensor(aa[:, 0:ON_GPSIMD], a_head[:], kp[:, 0:ON_GPSIMD], ALU.mult)
+        nc.vector.tensor_tensor(aa[:, ON_GPSIMD:BANK], a_acc[0][:, ON_GPSIMD:BANK], kp[:, ON_GPSIMD:BANK], ALU.mult)
+        nc.vector.tensor_tensor(aa[:, BANK:T], a_acc[1][:], kp[:, BANK:T], ALU.mult)
 
         for h in range(2):
             entries = slice(h * half_cols, (h + 1) * half_cols)
-            a3 = sb.tile([P, half_slots], F32)
+            a3 = sb.tile([P, half_slots], F32, tag="a3_then_b_head")
             nc.vector.tensor_copy(a3[:], aa[:].indirect(l3[:, entries]))
             v = sb.tile([P, half_slots], F32, name="v%d" % h)
             nc.vector.tensor_tensor(v[:], a3[:], b4[h][:], ALU.max)
             nc.scalar.activation(f1[:].indirect(l4[:, entries]), v[:], ACT.Copy)
 
+        b_head = sb.tile([P, ON_GPSIMD], F32, tag="a3_then_b_head")
+        nc.vector.tensor_copy(b_head[:, 0:B_PIECE], b_acc[0][:])
+        nc.vector.tensor_copy(b_head[:, B_PIECE:ON_GPSIMD], b_acc[1][:, 0 : ON_GPSIMD - B_PIECE])
         bb = sb.tile([P, U], F32)
-        for i in range(U // B_PIECE):
-            cols = slice(i * B_PIECE, (i + 1) * B_PIECE)
-            nc.vector.tensor_tensor(bb[:, cols], f1[:, cols], b_acc[i][:], ALU.subtract)
+        nc.gpsimd.tensor_tensor(bb[:, 0:ON_GPSIMD], f1[:, 0:ON_GPSIMD], b_head[:], ALU.subtract)
+        for i in range(1, U // B_PIECE):
+            u0 = max(i * B_PIECE, ON_GPSIMD)
+            u1 = (i + 1) * B_PIECE
+            nc.vector.tensor_tensor(bb[:, u0:u1], f1[:, u0:u1], b_acc[i][:, u0 - i * B_PIECE : B_PIECE], ALU.subtract)
 
         y0 = sb.tile([P, half_slots], F32)
         nc.vector.tensor_copy(y0[:], bb[:].indirect(l5[:, 0:half_cols]))

@@ -19,17 +19,17 @@ ACT = mybir.ActivationFunctionType
 
 P = 128
 PACK = 4
-LIST_COLS = SLOTS // 16
+QUADRANT = 32
+SCALE_ROWS = 4
 BANK = 512
+LIST_COLS = SLOTS // 16
+HALF_SLOTS = SLOTS // 2
+HALF_COLS = LIST_COLS // 2
 B_PIECE = 256
+B_PIECE_ON_VECTOR = 2
 CAST_ON_VECTOR = 72
-ON_GPSIMD = 320
-
-
-def load_scale_rows(engines, plane, scales):
-    by_row = scales[0].rearrange("(g r) n -> r g n", r=4)
-    for r, engine in enumerate(engines):
-        engine.dma_start(plane[r:P:32, :].bitcast(I32), by_row[r].bitcast(I32))
+AA_ON_GPSIMD = 352
+BB_ON_GPSIMD = 384
 
 
 def tile_attend_softkeep_side_kernel(tc, states, wq_words, wq_scales, cache_words, cache_scales, draft_words,
@@ -39,7 +39,7 @@ def tile_attend_softkeep_side_kernel(tc, states, wq_words, wq_scales, cache_word
         sb = ctx.enter_context(tc.tile_pool(name="sb", bufs=1))
         ps = ctx.enter_context(tc.psum_pool(name="ps", bufs=1))
 
-        draft_plane = sb.tile([P, U], U8, align_bytes=64)
+        draft_plane = sb.tile([P, B_PIECE], U8, align_bytes=64)
         wq_plane = sb.tile([P, K], U8, align_bytes=64)
         cache_plane = sb.tile([P, T], U8, align_bytes=64)
         kp = sb.tile([P, T], F32)
@@ -53,34 +53,40 @@ def tile_attend_softkeep_side_kernel(tc, states, wq_words, wq_scales, cache_word
 
         raw = sb.tile([P, PACK, Q], F32)
         nc.sync.dma_start(raw[:], states.rearrange("(p j) q -> p j q", j=PACK))
-        load_scale_rows((nc.scalar, nc.scalar, nc.sync, nc.sync), draft_plane, draft_scales)
+        pieces = U // B_PIECE
+        by_quadrant = draft_scales[0].bitcast(I32).rearrange("(g r) (i n) -> g i r n", r=SCALE_ROWS, i=pieces)
+        for g, engine in enumerate((nc.scalar, nc.scalar, nc.sync, nc.sync)):
+            rows = slice(QUADRANT * g, QUADRANT * g + pieces * SCALE_ROWS)
+            engine.dma_start(draft_plane[rows, :].bitcast(I32), by_quadrant[g])
         draft_rows = draft_words[0].rearrange("p n t -> p (n t)").bitcast(I32)
         draft = []
-        for h in range(U // BANK):
-            half = sb.tile([P, BANK], U32, align_bytes=64, name="draft%d" % h)
-            nc.sync.dma_start(half[:].bitcast(I32), draft_rows[:, h * BANK : (h + 1) * BANK])
-            draft.append(half)
-        wq_rows = sb.tile([4, 4, K // 4], I32)
-        nc.sync.dma_start(wq_rows[:], wq_scales[0].bitcast(I32).rearrange("(g r) n -> r g n", r=4))
-        wq = sb.tile([P, K], U32, align_bytes=64, tag="wq_then_b4")
-        nc.sync.dma_start(wq[:].bitcast(I32), wq_words[0].rearrange("p n t -> p (n t)").bitcast(I32))
-        l1 = sb.tile([P, LIST_COLS], U16)
-        nc.sync.dma_start(l1[:], offs)
+        for half in range(U // BANK):
+            words = sb.tile([P, BANK], U32, align_bytes=64, name="draft%d" % half)
+            nc.sync.dma_start(words[:].bitcast(I32), draft_rows[:, half * BANK : (half + 1) * BANK])
+            draft.append(words)
+        wq_rows = sb.tile([SCALE_ROWS, P // QUADRANT, K // 4], I32)
+        nc.sync.dma_start(wq_rows[:], wq_scales[0].bitcast(I32).rearrange("(g r) n -> r g n", r=SCALE_ROWS))
         thr_sb = sb.tile([P, 1], F32)
         nc.sync.dma_start(thr_sb[:], thr)
         slope_sb = sb.tile([P, 1], F32)
         nc.sync.dma_start(slope_sb[:], slope)
-        l2 = sb.tile([P, LIST_COLS], U16)
-        nc.sync.dma_start(l2[:], offs2)
-        l4 = sb.tile([P, LIST_COLS], U16)
-        nc.sync.dma_start(l4[:], offs4)
+        list1 = sb.tile([P, LIST_COLS], U16)
+        nc.sync.dma_start(list1[:], offs)
+        wq = sb.tile([P, K], U32, align_bytes=64, tag="wq_then_b4")
+        nc.sync.dma_start(wq[:].bitcast(I32), wq_words[0].rearrange("p n t -> p (n t)").bitcast(I32))
+        list2 = sb.tile([P, LIST_COLS], U16)
+        nc.sync.dma_start(list2[:], offs2)
+        list4 = sb.tile([P, LIST_COLS], U16)
+        nc.sync.dma_start(list4[:], offs4)
         cache = sb.tile([P, 2 * T], U8, align_bytes=64)
         nc.sync.dma_start(cache[:].bitcast(I32), cache_words[0].bitcast(I32))
-        load_scale_rows((nc.sync,) * 4, cache_plane, cache_scales)
-        l3 = sb.tile([P, LIST_COLS], U16)
-        nc.sync.dma_start(l3[:], offs3)
-        l5 = sb.tile([P, LIST_COLS], U16)
-        nc.sync.dma_start(l5[:], offs5)
+        by_row = cache_scales[0].rearrange("(g r) n -> r g n", r=SCALE_ROWS)
+        for r in range(SCALE_ROWS):
+            nc.sync.dma_start(cache_plane[r:P:QUADRANT, :].bitcast(I32), by_row[r].bitcast(I32))
+        list3 = sb.tile([P, LIST_COLS], U16)
+        nc.sync.dma_start(list3[:], offs3)
+        list5 = sb.tile([P, LIST_COLS], U16)
+        nc.sync.dma_start(list5[:], offs5)
 
         warm_in = sb.tile([P, 1], F32)
         nc.gpsimd.memset(warm_in[:], 0.0)
@@ -96,90 +102,87 @@ def tile_attend_softkeep_side_kernel(tc, states, wq_words, wq_scales, cache_word
         nc.vector.quantize_mx(out=st_codes[:].bitcast(FP8X4), scales=st_plane[:],
                               in_=st16[:].rearrange("p q j -> p (q j)"))
 
-        for g in range(4):
-            nc.vector.tensor_copy(wq_plane[32 * g : 32 * g + 4, :].bitcast(I32), wq_rows[:, g, :])
+        for g in range(P // QUADRANT):
+            rows = slice(QUADRANT * g, QUADRANT * g + SCALE_ROWS)
+            nc.vector.tensor_copy(wq_plane[rows, :].bitcast(I32), wq_rows[:, g, :])
 
         b = sb.tile([P, U], F32, tag="b_then_aa")
         b_acc = []
-        for i in range(U // B_PIECE):
-            u0 = i * B_PIECE
-            h, c0 = divmod(u0, BANK)
-            acc = ps.tile([P, B_PIECE], F32, name="b_acc%d" % i)
-            nc.tensor.matmul_mx(out=acc[:], lhsT=st_codes[:].bitcast(FP8X4), lhsT_scale=st_plane[:],
-                                rhs=draft[h][:, c0 : c0 + B_PIECE].bitcast(FP8X4),
-                                rhs_scale=draft_plane[:, u0 : u0 + B_PIECE], start=True, stop=True)
-            copy_out = nc.vector.tensor_copy if i % 2 == 0 else nc.scalar.copy
-            copy_out(b[:, u0 : u0 + B_PIECE], acc[:])
-            b_acc.append(acc)
+        for i in range(pieces):
+            half, col = divmod(i * B_PIECE, BANK)
+            bank = ps.tile([P, B_PIECE], F32, name="b_acc%d" % i)
+            nc.tensor.matmul_mx(out=bank[:], lhsT=st_codes[:].bitcast(FP8X4), lhsT_scale=st_plane[:],
+                                rhs=draft[half][:, col : col + B_PIECE].bitcast(FP8X4),
+                                rhs_scale=draft_plane[SCALE_ROWS * i : P, :], start=True, stop=True)
+            copy_out = nc.vector.tensor_copy if i == B_PIECE_ON_VECTOR else nc.scalar.copy
+            copy_out(b[:, i * B_PIECE : (i + 1) * B_PIECE], bank[:])
+            b_acc.append(bank)
 
         s1 = sb.tile([P, SLOTS], F32)
-        half_slots = SLOTS // 2
-        half_cols = LIST_COLS // 2
-        for h in range(2):
-            nc.scalar.activation(s1[:, h * half_slots : (h + 1) * half_slots],
-                                 b[:].indirect(l1[:, h * half_cols : (h + 1) * half_cols]),
-                                 ACT.Sigmoid, bias=thr_sb[:], scale=slope_sb[:])
-        for h in range(2):
-            nc.scalar.activation(kp[:].indirect(l2[:, h * half_cols : (h + 1) * half_cols]),
-                                 s1[:, h * half_slots : (h + 1) * half_slots], ACT.Copy)
+        nc.scalar.activation(s1[:], b[:].indirect(list1[:]), ACT.Sigmoid, bias=thr_sb[:], scale=slope_sb[:])
+        nc.scalar.activation(kp[:].indirect(list2[:]), s1[:], ACT.Copy)
 
         qv_acc = ps.tile([P, K], F32)
         nc.tensor.matmul_mx(out=qv_acc[:], lhsT=st_codes[:].bitcast(FP8X4), lhsT_scale=st_plane[:],
                             rhs=wq[:].bitcast(FP8X4), rhs_scale=wq_plane[:], start=True, stop=True)
         qv_turned = ps.tile([P, 2, Q], F32)
-        for u in range(2):
-            qv_rows = sb.tile([P, P, 2], BF16, name="qv_rows%d" % u)
-            nc.vector.tensor_copy(qv_rows[:], qv_acc[:].rearrange("q (p u e) -> q u p e", u=2, e=2)[:, u])
-            nc.tensor.transpose(qv_turned[:, u, :], qv_rows[:].rearrange("q p e -> q (p e)").bitcast(F32), ident[:])
+        by_pair = qv_acc[:].rearrange("q (p pair e) -> q pair p e", pair=2, e=2)
+        for pair in range(2):
+            qv_words = sb.tile([P, P, 2], BF16, name="qv_words%d" % pair)
+            nc.vector.tensor_copy(qv_words[:], by_pair[:, pair])
+            nc.tensor.transpose(qv_turned[:, pair, :], qv_words[:].rearrange("q p e -> q (p e)").bitcast(F32),
+                                ident[:])
         qv16 = sb.tile([P, Q * PACK], BF16, align_bytes=64, tag="qv16_then_b4")
-        nc.vector.tensor_copy(qv16[:].bitcast(F32).rearrange("p (q u) -> p q u", u=2),
-                              qv_turned[:].rearrange("p u q -> p q u"))
+        nc.vector.tensor_copy(qv16[:].bitcast(F32).rearrange("p (q pair) -> p q pair", pair=2),
+                              qv_turned[:].rearrange("p pair q -> p q pair"))
         qv_codes = sb.tile([P, Q], U32, align_bytes=64)
         qv_plane = sb.tile([P, Q], U8, align_bytes=64)
-        nc.vector.quantize_mx(out=qv_codes[:].bitcast(FP8X4), scales=qv_plane[:],
-                              in_=qv16[:])
+        nc.vector.quantize_mx(out=qv_codes[:].bitcast(FP8X4), scales=qv_plane[:], in_=qv16[:])
         a_acc = []
-        for h in range(T // BANK):
-            acc = ps.tile([P, BANK], F32, name="a_acc%d" % h)
-            nc.tensor.matmul_mx(out=acc[:], lhsT=qv_codes[:].bitcast(FP8X4), lhsT_scale=qv_plane[:],
-                                rhs=cache[:, 2 * h * BANK : 2 * (h + 1) * BANK].bitcast(FP4X4),
-                                rhs_scale=cache_plane[:, h * BANK : (h + 1) * BANK], start=True, stop=True)
-            a_acc.append(acc)
+        for half in range(T // BANK):
+            bank = ps.tile([P, BANK], F32, name="a_acc%d" % half)
+            nc.tensor.matmul_mx(out=bank[:], lhsT=qv_codes[:].bitcast(FP8X4), lhsT_scale=qv_plane[:],
+                                rhs=cache[:, 2 * half * BANK : 2 * (half + 1) * BANK].bitcast(FP4X4),
+                                rhs_scale=cache_plane[:, half * BANK : (half + 1) * BANK], start=True, stop=True)
+            a_acc.append(bank)
 
         b4 = []
-        for h, tag in enumerate(("wq_then_b4", "qv16_then_b4")):
-            piece = sb.tile([P, half_slots], F32, align_bytes=64, name="b4_%d" % h, tag=tag)
-            nc.vector.tensor_copy(piece[:], b[:].indirect(l4[:, h * half_cols : (h + 1) * half_cols]))
-            b4.append(piece)
+        for half, tag in enumerate(("wq_then_b4", "qv16_then_b4")):
+            looked_up = sb.tile([P, HALF_SLOTS], F32, align_bytes=64, name="b4_%d" % half, tag=tag)
+            nc.vector.tensor_copy(looked_up[:], b[:].indirect(list4[:, half * HALF_COLS : (half + 1) * HALF_COLS]))
+            b4.append(looked_up)
 
-        a_head = sb.tile([P, ON_GPSIMD], F32)
-        nc.vector.tensor_copy(a_head[:], a_acc[0][:, 0:ON_GPSIMD])
+        a_head = sb.tile([P, AA_ON_GPSIMD], F32)
+        nc.vector.tensor_copy(a_head[:], a_acc[0][:, 0:AA_ON_GPSIMD])
         aa = sb.tile([P, T], F32, tag="b_then_aa")
-        nc.gpsimd.tensor_tensor(aa[:, 0:ON_GPSIMD], a_head[:], kp[:, 0:ON_GPSIMD], ALU.mult)
-        nc.vector.tensor_tensor(aa[:, ON_GPSIMD:BANK], a_acc[0][:, ON_GPSIMD:BANK], kp[:, ON_GPSIMD:BANK], ALU.mult)
+        nc.gpsimd.tensor_tensor(aa[:, 0:AA_ON_GPSIMD], a_head[:], kp[:, 0:AA_ON_GPSIMD], ALU.mult)
+        nc.vector.tensor_tensor(aa[:, AA_ON_GPSIMD:BANK], a_acc[0][:, AA_ON_GPSIMD:BANK],
+                                kp[:, AA_ON_GPSIMD:BANK], ALU.mult)
         nc.vector.tensor_tensor(aa[:, BANK:T], a_acc[1][:], kp[:, BANK:T], ALU.mult)
 
-        for h in range(2):
-            entries = slice(h * half_cols, (h + 1) * half_cols)
-            a3 = sb.tile([P, half_slots], F32, tag="a3_then_b_head")
-            nc.vector.tensor_copy(a3[:], aa[:].indirect(l3[:, entries]))
-            v = sb.tile([P, half_slots], F32, name="v%d" % h)
-            nc.vector.tensor_tensor(v[:], a3[:], b4[h][:], ALU.max)
-            nc.scalar.activation(f1[:].indirect(l4[:, entries]), v[:], ACT.Copy)
+        a3_first = sb.tile([P, HALF_SLOTS], F32)
+        nc.vector.tensor_copy(a3_first[:], aa[:].indirect(list3[:, 0:HALF_COLS]))
+        a3_second = sb.tile([P, HALF_SLOTS], F32, tag="a3_then_b_head")
+        nc.scalar.activation(a3_second[:], aa[:].indirect(list3[:, HALF_COLS:LIST_COLS]), ACT.Copy)
+        v = sb.tile([P, SLOTS], F32)
+        for half, a3 in enumerate((a3_first, a3_second)):
+            nc.vector.tensor_tensor(v[:, half * HALF_SLOTS : (half + 1) * HALF_SLOTS], a3[:], b4[half][:], ALU.max)
+        nc.scalar.activation(f1[:].indirect(list4[:]), v[:], ACT.Copy)
 
-        b_head = sb.tile([P, ON_GPSIMD], F32, tag="a3_then_b_head")
+        b_head = sb.tile([P, BB_ON_GPSIMD], F32, tag="a3_then_b_head")
         nc.vector.tensor_copy(b_head[:, 0:B_PIECE], b_acc[0][:])
-        nc.vector.tensor_copy(b_head[:, B_PIECE:ON_GPSIMD], b_acc[1][:, 0 : ON_GPSIMD - B_PIECE])
+        nc.vector.tensor_copy(b_head[:, B_PIECE:BB_ON_GPSIMD], b_acc[1][:, 0 : BB_ON_GPSIMD - B_PIECE])
         bb = sb.tile([P, U], F32)
-        nc.gpsimd.tensor_tensor(bb[:, 0:ON_GPSIMD], f1[:, 0:ON_GPSIMD], b_head[:], ALU.subtract)
-        for i in range(1, U // B_PIECE):
-            u0 = max(i * B_PIECE, ON_GPSIMD)
-            u1 = (i + 1) * B_PIECE
-            nc.vector.tensor_tensor(bb[:, u0:u1], f1[:, u0:u1], b_acc[i][:, u0 - i * B_PIECE : B_PIECE], ALU.subtract)
+        nc.gpsimd.tensor_tensor(bb[:, 0:BB_ON_GPSIMD], f1[:, 0:BB_ON_GPSIMD], b_head[:], ALU.subtract)
+        for i in range(1, pieces):
+            first = max(i * B_PIECE, BB_ON_GPSIMD)
+            end = (i + 1) * B_PIECE
+            nc.vector.tensor_tensor(bb[:, first:end], f1[:, first:end], b_acc[i][:, first - i * B_PIECE : B_PIECE],
+                                    ALU.subtract)
 
-        y0 = sb.tile([P, half_slots], F32)
-        nc.vector.tensor_copy(y0[:], bb[:].indirect(l5[:, 0:half_cols]))
-        nc.sync.dma_start(out[:, 0:half_slots], y0[:])
-        y1 = sb.tile([P, half_slots], F32)
-        nc.scalar.activation(y1[:], bb[:].indirect(l5[:, half_cols:LIST_COLS]), ACT.Copy)
-        nc.scalar.dma_start(out[:, half_slots:SLOTS], y1[:])
+        y_first = sb.tile([P, HALF_SLOTS], F32)
+        nc.vector.tensor_copy(y_first[:], bb[:].indirect(list5[:, 0:HALF_COLS]))
+        nc.sync.dma_start(out[:, 0:HALF_SLOTS], y_first[:])
+        y_second = sb.tile([P, HALF_SLOTS], F32)
+        nc.scalar.activation(y_second[:], bb[:].indirect(list5[:, HALF_COLS:LIST_COLS]), ACT.Copy)
+        nc.scalar.dma_start(out[:, HALF_SLOTS:SLOTS], y_second[:])

from contextlib import ExitStack

import concourse.mybir as mybir
from concourse.masks import make_identity

D, K, T, U, SLOTS, Q = 512, 512, 1024, 1024, 512, 128
FLOPS = 2 * Q * (D * K + K * T + D * U)

F32 = mybir.dt.float32
BF16 = mybir.dt.bfloat16
I32 = mybir.dt.int32
U32 = mybir.dt.uint32
U16 = mybir.dt.uint16
U8 = mybir.dt.uint8
FP8X4 = mybir.dt.float8_e4m3fn_x4
FP4X4 = mybir.dt.float4_e2m1fn_x4
ALU = mybir.AluOpType
ACT = mybir.ActivationFunctionType

P = 128
PACK = 4
QUADRANT = 32
SCALE_ROWS = 4
BANK = 512
LIST_COLS = SLOTS // 16
HALF_SLOTS = SLOTS // 2
HALF_COLS = LIST_COLS // 2
B_PIECE = 256
B_PIECE_ON_VECTOR = 2
CAST_ON_VECTOR = 72
AA_ON_GPSIMD = 352
BB_ON_GPSIMD = 384


def tile_attend_softkeep_side_kernel(tc, states, wq_words, wq_scales, cache_words, cache_scales, draft_words,
                                      draft_scales, thr, slope, offs, offs2, offs3, offs4, offs5, out):
    nc = tc.nc
    with ExitStack() as ctx:
        sb = ctx.enter_context(tc.tile_pool(name="sb", bufs=1))
        ps = ctx.enter_context(tc.psum_pool(name="ps", bufs=1))

        draft_plane = sb.tile([P, B_PIECE], U8, align_bytes=64)
        wq_plane = sb.tile([P, K], U8, align_bytes=64)
        cache_plane = sb.tile([P, T], U8, align_bytes=64)
        kp = sb.tile([P, T], F32)
        for plane in (draft_plane, wq_plane, cache_plane):
            nc.gpsimd.memset(plane[:].bitcast(I32), 0)
        nc.vector.memset(kp[:], 0.0)
        f1 = sb.tile([P, U], F32)
        nc.vector.memset(f1[:], 0.0)
        ident = sb.tile([P, P], F32)
        make_identity(nc, ident[:])

        raw = sb.tile([P, PACK, Q], F32)
        nc.sync.dma_start(raw[:], states.rearrange("(p j) q -> p j q", j=PACK))
        pieces = U // B_PIECE
        by_quadrant = draft_scales[0].bitcast(I32).rearrange("(g r) (i n) -> g i r n", r=SCALE_ROWS, i=pieces)
        for g, engine in enumerate((nc.scalar, nc.scalar, nc.sync, nc.sync)):
            rows = slice(QUADRANT * g, QUADRANT * g + pieces * SCALE_ROWS)
            engine.dma_start(draft_plane[rows, :].bitcast(I32), by_quadrant[g])
        draft_rows = draft_words[0].rearrange("p n t -> p (n t)").bitcast(I32)
        draft = []
        for half in range(U // BANK):
            words = sb.tile([P, BANK], U32, align_bytes=64, name="draft%d" % half)
            nc.sync.dma_start(words[:].bitcast(I32), draft_rows[:, half * BANK : (half + 1) * BANK])
            draft.append(words)
        wq_rows = sb.tile([SCALE_ROWS, P // QUADRANT, K // 4], I32)
        nc.sync.dma_start(wq_rows[:], wq_scales[0].bitcast(I32).rearrange("(g r) n -> r g n", r=SCALE_ROWS))
        thr_sb = sb.tile([P, 1], F32)
        nc.sync.dma_start(thr_sb[:], thr)
        slope_sb = sb.tile([P, 1], F32)
        nc.sync.dma_start(slope_sb[:], slope)
        list1 = sb.tile([P, LIST_COLS], U16)
        nc.sync.dma_start(list1[:], offs)
        wq = sb.tile([P, K], U32, align_bytes=64, tag="wq_then_b4")
        nc.sync.dma_start(wq[:].bitcast(I32), wq_words[0].rearrange("p n t -> p (n t)").bitcast(I32))
        list2 = sb.tile([P, LIST_COLS], U16)
        nc.sync.dma_start(list2[:], offs2)
        list4 = sb.tile([P, LIST_COLS], U16)
        nc.sync.dma_start(list4[:], offs4)
        cache = sb.tile([P, 2 * T], U8, align_bytes=64)
        nc.sync.dma_start(cache[:].bitcast(I32), cache_words[0].bitcast(I32))
        by_row = cache_scales[0].rearrange("(g r) n -> r g n", r=SCALE_ROWS)
        for r in range(SCALE_ROWS):
            nc.sync.dma_start(cache_plane[r:P:QUADRANT, :].bitcast(I32), by_row[r].bitcast(I32))
        list3 = sb.tile([P, LIST_COLS], U16)
        nc.sync.dma_start(list3[:], offs3)
        list5 = sb.tile([P, LIST_COLS], U16)
        nc.sync.dma_start(list5[:], offs5)

        warm_in = sb.tile([P, 1], F32)
        nc.gpsimd.memset(warm_in[:], 0.0)
        warm_out = sb.tile([P, 1], F32)
        nc.scalar.activation(warm_out[:], warm_in[:], ACT.Sigmoid)

        st16 = sb.tile([P, Q, PACK], BF16, align_bytes=64)
        by_query = raw[:].rearrange("p j q -> p q j")
        nc.vector.tensor_copy(st16[:, 0:CAST_ON_VECTOR, :], by_query[:, 0:CAST_ON_VECTOR, :])
        nc.scalar.copy(st16[:, CAST_ON_VECTOR:Q, :], by_query[:, CAST_ON_VECTOR:Q, :])
        st_codes = sb.tile([P, Q], U32, align_bytes=64)
        st_plane = sb.tile([P, Q], U8, align_bytes=64)
        nc.vector.quantize_mx(out=st_codes[:].bitcast(FP8X4), scales=st_plane[:],
                              in_=st16[:].rearrange("p q j -> p (q j)"))

        for g in range(P // QUADRANT):
            rows = slice(QUADRANT * g, QUADRANT * g + SCALE_ROWS)
            nc.vector.tensor_copy(wq_plane[rows, :].bitcast(I32), wq_rows[:, g, :])

        b = sb.tile([P, U], F32, tag="b_then_aa")
        b_acc = []
        for i in range(pieces):
            half, col = divmod(i * B_PIECE, BANK)
            bank = ps.tile([P, B_PIECE], F32, name="b_acc%d" % i)
            nc.tensor.matmul_mx(out=bank[:], lhsT=st_codes[:].bitcast(FP8X4), lhsT_scale=st_plane[:],
                                rhs=draft[half][:, col : col + B_PIECE].bitcast(FP8X4),
                                rhs_scale=draft_plane[SCALE_ROWS * i : P, :], start=True, stop=True)
            copy_out = nc.vector.tensor_copy if i == B_PIECE_ON_VECTOR else nc.scalar.copy
            copy_out(b[:, i * B_PIECE : (i + 1) * B_PIECE], bank[:])
            b_acc.append(bank)

        s1 = sb.tile([P, SLOTS], F32)
        nc.scalar.activation(s1[:], b[:].indirect(list1[:]), ACT.Sigmoid, bias=thr_sb[:], scale=slope_sb[:])
        nc.scalar.activation(kp[:].indirect(list2[:]), s1[:], ACT.Copy)

        qv_acc = ps.tile([P, K], F32)
        nc.tensor.matmul_mx(out=qv_acc[:], lhsT=st_codes[:].bitcast(FP8X4), lhsT_scale=st_plane[:],
                            rhs=wq[:].bitcast(FP8X4), rhs_scale=wq_plane[:], start=True, stop=True)
        qv_turned = ps.tile([P, 2, Q], F32)
        by_pair = qv_acc[:].rearrange("q (p pair e) -> q pair p e", pair=2, e=2)
        for pair in range(2):
            qv_words = sb.tile([P, P, 2], BF16, name="qv_words%d" % pair)
            nc.vector.tensor_copy(qv_words[:], by_pair[:, pair])
            nc.tensor.transpose(qv_turned[:, pair, :], qv_words[:].rearrange("q p e -> q (p e)").bitcast(F32),
                                ident[:])
        qv16 = sb.tile([P, Q * PACK], BF16, align_bytes=64, tag="qv16_then_b4")
        nc.vector.tensor_copy(qv16[:].bitcast(F32).rearrange("p (q pair) -> p q pair", pair=2),
                              qv_turned[:].rearrange("p pair q -> p q pair"))
        qv_codes = sb.tile([P, Q], U32, align_bytes=64)
        qv_plane = sb.tile([P, Q], U8, align_bytes=64)
        nc.vector.quantize_mx(out=qv_codes[:].bitcast(FP8X4), scales=qv_plane[:], in_=qv16[:])
        a_acc = []
        for half in range(T // BANK):
            bank = ps.tile([P, BANK], F32, name="a_acc%d" % half)
            nc.tensor.matmul_mx(out=bank[:], lhsT=qv_codes[:].bitcast(FP8X4), lhsT_scale=qv_plane[:],
                                rhs=cache[:, 2 * half * BANK : 2 * (half + 1) * BANK].bitcast(FP4X4),
                                rhs_scale=cache_plane[:, half * BANK : (half + 1) * BANK], start=True, stop=True)
            a_acc.append(bank)

        b4 = []
        for half, tag in enumerate(("wq_then_b4", "qv16_then_b4")):
            looked_up = sb.tile([P, HALF_SLOTS], F32, align_bytes=64, name="b4_%d" % half, tag=tag)
            nc.vector.tensor_copy(looked_up[:], b[:].indirect(list4[:, half * HALF_COLS : (half + 1) * HALF_COLS]))
            b4.append(looked_up)

        a_head = sb.tile([P, AA_ON_GPSIMD], F32)
        nc.vector.tensor_copy(a_head[:], a_acc[0][:, 0:AA_ON_GPSIMD])
        aa = sb.tile([P, T], F32, tag="b_then_aa")
        nc.gpsimd.tensor_tensor(aa[:, 0:AA_ON_GPSIMD], a_head[:], kp[:, 0:AA_ON_GPSIMD], ALU.mult)
        nc.vector.tensor_tensor(aa[:, AA_ON_GPSIMD:BANK], a_acc[0][:, AA_ON_GPSIMD:BANK],
                                kp[:, AA_ON_GPSIMD:BANK], ALU.mult)
        nc.vector.tensor_tensor(aa[:, BANK:T], a_acc[1][:], kp[:, BANK:T], ALU.mult)

        a3_first = sb.tile([P, HALF_SLOTS], F32)
        nc.vector.tensor_copy(a3_first[:], aa[:].indirect(list3[:, 0:HALF_COLS]))
        a3_second = sb.tile([P, HALF_SLOTS], F32, tag="a3_then_b_head")
        nc.scalar.activation(a3_second[:], aa[:].indirect(list3[:, HALF_COLS:LIST_COLS]), ACT.Copy)
        v = sb.tile([P, SLOTS], F32)
        for half, a3 in enumerate((a3_first, a3_second)):
            nc.vector.tensor_tensor(v[:, half * HALF_SLOTS : (half + 1) * HALF_SLOTS], a3[:], b4[half][:], ALU.max)
        nc.scalar.activation(f1[:].indirect(list4[:]), v[:], ACT.Copy)

        b_head = sb.tile([P, BB_ON_GPSIMD], F32, tag="a3_then_b_head")
        nc.vector.tensor_copy(b_head[:, 0:B_PIECE], b_acc[0][:])
        nc.vector.tensor_copy(b_head[:, B_PIECE:BB_ON_GPSIMD], b_acc[1][:, 0 : BB_ON_GPSIMD - B_PIECE])
        bb = sb.tile([P, U], F32)
        nc.gpsimd.tensor_tensor(bb[:, 0:BB_ON_GPSIMD], f1[:, 0:BB_ON_GPSIMD], b_head[:], ALU.subtract)
        for i in range(1, pieces):
            first = max(i * B_PIECE, BB_ON_GPSIMD)
            end = (i + 1) * B_PIECE
            nc.vector.tensor_tensor(bb[:, first:end], f1[:, first:end], b_acc[i][:, first - i * B_PIECE : B_PIECE],
                                    ALU.subtract)

        y_first = sb.tile([P, HALF_SLOTS], F32)
        nc.vector.tensor_copy(y_first[:], bb[:].indirect(list5[:, 0:HALF_COLS]))
        nc.sync.dma_start(out[:, 0:HALF_SLOTS], y_first[:])
        y_second = sb.tile([P, HALF_SLOTS], F32)
        nc.scalar.activation(y_second[:], bb[:].indirect(list5[:, HALF_COLS:LIST_COLS]), ACT.Copy)
        nc.scalar.dma_start(out[:, HALF_SLOTS:SLOTS], y_second[:])
